import numpy as np
import ml_dtypes


def mxq(x, axis, fmt="e4m3"):
    dtype, down = {"e4m3": (ml_dtypes.float8_e4m3fn, 7), "e5m2": (ml_dtypes.float8_e5m2, 14)}[fmt]
    v = np.moveaxis(np.asarray(x, np.float32).astype(ml_dtypes.bfloat16).astype(np.float64), axis, -1)
    blocks = v.reshape(v.shape[:-1] + (-1, 32))
    amax = np.abs(blocks).max(-1, keepdims=True)
    byte = np.maximum(np.where(amax > 0, np.frexp(amax)[1] - 1 + 127, 0) - down, 1)
    scale = np.exp2(byte - 127.0)
    codes = (blocks / scale).astype(np.float32).astype(dtype).astype(np.float64)
    return np.moveaxis((codes * scale).reshape(v.shape), -1, axis)


WIDE = False


def mx_kscale(k):
    if not WIDE:
        return np.ones(k)
    levels = np.array([10, -10, 5, -5, 0])
    if k % 512:
        return np.exp2(np.random.permutation(np.resize(levels, k // 32))).repeat(32)
    a = np.empty((k // 512, 16))
    for p in range(k // 512):
        a[p, :8] = np.random.permutation(np.resize(levels, 8))
        for g in range(8):
            far = levels[np.abs(levels - a[p, g]) >= 10]
            a[p, g + 8] = far[np.random.randint(len(far))]
    return np.exp2(a.ravel()).repeat(32)


def f64(x):
    return np.asarray(x).astype(np.float64)


def striped(idx):
    return np.tile(idx.reshape(-1, 16).T, (8, 1)).astype(np.uint16)


def unstriped(offs):
    return offs[:16].T.reshape(-1).astype(np.int64)


def gelu(v):
    return 0.5 * v * (1.0 + np.tanh(np.sqrt(2.0 / np.pi) * (v + 0.044715 * v**3)))


K, T, S, H, N = 1536, 1024, 512, 1024, 128


def setup_inputs():
    n = np.random.standard_normal
    s = mx_kscale(K)[:, None]
    u = mx_kscale(H)
    return {
        "xT": (n((K, T)) * s).astype(np.float32),
        "w1": (n((K, H)) / np.sqrt(K) / s).astype(np.float32),
        "w3": (n((K, H)) / np.sqrt(K) / s * u).astype(np.float32),
        "w2": (n((H, N)) / np.sqrt(H) / u[:, None]).astype(np.float32),
        "offs": striped(np.sort(np.random.permutation(T)[:S])),
    }


def reference(xT, w1, w3, w2, offs):
    idx = unstriped(offs)
    xq = mxq(f64(xT)[:, idx], 0, "e4m3")
    h = gelu(mxq(f64(w1), 0, "e4m3").T @ xq) * (mxq(f64(w3), 0, "e4m3").T @ xq)
    y = mxq(f64(w2), 0, "e4m3").T @ mxq(h, 0, "e4m3")
    return y

@@ -1,0 +1,267 @@
+from contextlib import ExitStack
+
+import concourse.mybir as mybir
+
+K, T, S, H, N = 1536, 1024, 512, 1024, 128
+FLOPS = 2 * K * H * S * 2 + 2 * H * N * S
+
+F32 = mybir.dt.float32
+BF16 = mybir.dt.bfloat16
+U32 = mybir.dt.uint32
+U16 = mybir.dt.uint16
+U8 = mybir.dt.uint8
+FP8X4 = mybir.dt.float8_e4m3fn_x4
+MULT = mybir.AluOpType.mult
+GELU = mybir.ActivationFunctionType.Gelu_apprx_tanh
+
+P = 128
+PACK = 4
+K_PASS = P * PACK
+PASSES = K // K_PASS
+HALF = 512
+HALVES = H // HALF
+BLOCK = 128
+BLOCKS = S // BLOCK
+
+X_SCALAR = [(256, 128), (448, 384), (448, 256)]
+W_SCALAR = [96, 96, 32, 16, 16, 48, 48, 64, 96, 32, 0]
+
+
+def copy_on(nc, on_scalar, dst, src):
+    if on_scalar:
+        nc.scalar.copy(out=dst, in_=src)
+    else:
+        nc.vector.tensor_copy(out=dst, in_=src)
+
+
+def interleave(nc, on_scalar, dst, src):
+    copy_on(
+        nc,
+        on_scalar,
+        dst.rearrange("p (c i) j -> p c j i", i=4),
+        src.rearrange("p j (c i) -> p c j i", i=4),
+    )
+
+
+def interleave_permuted(nc, on_scalar, dst, src, m0, m1):
+    copy_on(
+        nc,
+        on_scalar,
+        dst.rearrange("p (t m) j -> p m j t", t=4)[:, m0:m1],
+        src.rearrange("p j (m t) -> p m j t", t=4)[:, m0:m1],
+    )
+
+
+def quantize(nc, codes, scales, grouped):
+    nc.vector.quantize_mx(out=codes.bitcast(FP8X4), scales=scales, in_=grouped.rearrange("p w j -> p (w j)"))
+
+
+def mm(nc, out, w, col, x, n0, n, start, stop):
+    nc.tensor.matmul_mx(
+        out=out,
+        lhsT=w[0][:, col : col + P].bitcast(FP8X4),
+        lhsT_scale=w[1][:, col : col + P],
+        rhs=x[0][:, n0 : n0 + n].bitcast(FP8X4),
+        rhs_scale=x[1][:, n0 : n0 + n],
+        start=start,
+        stop=stop,
+    )
+
+
+def tile_picked_pick_glu_gelu_srt_e_kernel(tc, xT, w1, w3, w2, offs, out):
+    nc = tc.nc
+    with ExitStack() as ctx:
+        keep = ctx.enter_context(tc.tile_pool(name="keep", bufs=1))
+        raws = ctx.enter_context(tc.tile_pool(name="raws", bufs=1))
+        stage = ctx.enter_context(tc.tile_pool(name="stage", bufs=3))
+        psum = ctx.enter_context(tc.psum_pool(name="psum", bufs=8))
+
+        offsets = keep.tile([P, S // 16], U16, name="offsets")
+
+        x_view = xT.rearrange("(g p j) c -> g p j c", g=PASSES, j=PACK)
+        w_views = [w.rearrange("(g p j) c -> g p j c", g=PASSES, j=PACK) for w in (w1, w3)]
+        w2_view = w2.rearrange("(g p j) c -> p g j c", g=HALVES, j=PACK)
+
+        xr = []
+        for g in range(PASSES):
+            r = raws.tile([P, PACK, T], F32, name="rawx", bufs=3)
+            nc.sync.dma_start(out=r[:, :, 0:512], in_=x_view[g][:, :, 0:512])
+            nc.sync.dma_start(out=r[:, :, 512:1024], in_=x_view[g][:, :, 512:1024])
+            if g == 0:
+                nc.sync.dma_start(out=offsets[:], in_=offs)
+            xr.append(r)
+        chunks = [(h, k, g) for h in range(HALVES) for k in range(2) for g in range(PASSES)]
+        wr = {}
+        for h, k, g in chunks:
+            r = raws.tile([P, PACK, HALF], F32, name="raww", bufs=8)
+            c0 = h * HALF
+            if (h, k, g) == chunks[-1]:
+                nc.sync.dma_start(out=r[:, :, 0:256], in_=w_views[k][g][:, :, c0 : c0 + 256])
+                nc.sync.dma_start(out=r[:, :, 256:512], in_=w_views[k][g][:, :, c0 + 256 : c0 + 512])
+            else:
+                nc.sync.dma_start(out=r[:], in_=w_views[k][g][:, :, c0 : c0 + HALF])
+            wr[h, k, g] = r
+        w2r = keep.tile([P, HALVES, PACK, N], F32, name="w2r")
+        nc.sync.dma_start(out=w2r[:], in_=w2_view)
+
+        warm = keep.tile([P, 1], F32, name="warm")
+        nc.vector.memset(warm[:], 0.0)
+        nc.scalar.activation(warm[:], warm[:], GELU)
+
+        words, bytes8, picked = [], [], []
+        for g in range(PASSES):
+            words.append(keep.tile([P, T], U32, name=f"words{g}", align_bytes=64))
+            bytes8.append(keep.tile([P, T], U8, name=f"bytes{g}", align_bytes=64))
+            nc.gpsimd.memset(bytes8[g][:], 0)
+
+        def copy_x(g):
+            grouped = stage.tile([P, T, PACK], BF16, name="xg", align_bytes=64, bufs=2)
+            for a in range(0, T, 512):
+                b = a + X_SCALAR[g][a // 512]
+                interleave(nc, True, grouped[:, a:b, :], xr[g][:, :, a:b])
+                interleave(nc, False, grouped[:, b : a + 512, :], xr[g][:, :, b : a + 512])
+                quantize(nc, words[g][:, a : a + 512], bytes8[g][:, a : a + 512], grouped[:, a : a + 512, :])
+
+        def gather_x(g):
+            gw = keep.tile([P, S], U32, name=f"pw{g}", align_bytes=64)
+            gs = keep.tile([P, S], U8, name=f"ps{g}", align_bytes=64)
+            nc.vector.tensor_copy(gw[:], words[g][:].indirect(offsets[:]))
+            nc.vector.tensor_copy(gs[:], bytes8[g][:].indirect(offsets[:]))
+            picked.append((gw, gs))
+
+        wg = {}
+        wq = {}
+
+        def copy_w(h, k, g):
+            grouped = stage.tile([P, HALF, PACK], BF16, name="wg", align_bytes=64, bufs=4)
+            if (h, k, g) == chunks[-1]:
+                splits = [(True, 0, 16), (False, 16, 64), (True, 64, 80), (False, 80, 128)]
+            else:
+                m = W_SCALAR[chunks.index((h, k, g))]
+                splits = [(on, a, b) for on, a, b in ((True, 0, m), (False, m, P)) if a < b]
+            for on_scalar, m0, m1 in splits:
+                interleave_permuted(nc, on_scalar, grouped[:], wr[h, k, g][:], m0, m1)
+            wg[h, k, g] = grouped
+
+        def quantize_w(h, k, g):
+            codes = keep.tile([P, HALF], U32, name=f"wc{h}{k}{g}", align_bytes=64)
+            scales = keep.tile([P, HALF], U8, name=f"ws{h}{k}{g}", align_bytes=64)
+            quantize(nc, codes[:], scales[:], wg[h, k, g][:])
+            wq[h, k, g] = (codes, scales)
+
+        acc = {}
+        gate = {}
+        banks = {}
+        hg = {}
+        hq = {}
+
+        def products1(h, g):
+            for t in range(PACK):
+                if g == 0:
+                    acc[h, t] = psum.tile([P, S], F32, name="bank")
+                mm(nc, acc[h, t][:], wq[h, 0, g], t * P, picked[g], 0, S, g == 0, g == PASSES - 1)
+
+        def gelus(h):
+            gate[h] = keep.tile([P, PACK, S], F32, name=f"gate{h}")
+            for t in range(PACK):
+                nc.scalar.activation(gate[h][:, t, :], acc[h, t][:], GELU)
+
+        def products3_early(h):
+            for b in range(BLOCKS):
+                banks[h, b] = psum.tile([P, PACK, BLOCK], F32, name="bank")
+                for g in range(PASSES - 1):
+                    mm(nc, banks[h, b][:, 0, :], wq[h, 1, g], 0, picked[g], b * BLOCK, BLOCK, g == 0, False)
+
+        def products3(h, b):
+            for t in range(PACK):
+                for g in range(PASSES - 1 if t == 0 else 0, PASSES):
+                    mm(nc, banks[h, b][:, t, :], wq[h, 1, g], t * P, picked[g], b * BLOCK, BLOCK, g == 0, g == PASSES - 1)
+
+        def multiply(h, b):
+            n = slice(b * BLOCK, (b + 1) * BLOCK)
+            if b == 0:
+                hg[h] = keep.tile([P, S, PACK], BF16, name=f"hg{h}", align_bytes=64)
+                hq[h] = (
+                    keep.tile([P, S], U32, name=f"hc{h}", align_bytes=64),
+                    keep.tile([P, S], U8, name=f"hs{h}", align_bytes=64),
+                )
+            nc.vector.tensor_tensor(
+                hg[h][:, n, :],
+                banks[h, b][:].rearrange("p t n -> p n t"),
+                gate[h][:, :, n].rearrange("p t n -> p n t"),
+                MULT,
+            )
+
+        def quantize_h(h, n0, n1):
+            quantize(nc, hq[h][0][:, n0:n1], hq[h][1][:, n0:n1], hg[h][:, n0:n1, :])
+
+        def keep_warm(n):
+            bank = psum.tile([P, S], F32, name="bank")
+            for _ in range(n):
+                mm(nc, bank[:], wq[1, 0, 0], 0, picked[0], 0, S, True, True)
+
+        for g in range(PASSES):
+            copy_x(g)
+            gather_x(g)
+        for g in range(PASSES):
+            copy_w(0, 0, g)
+            quantize_w(0, 0, g)
+            products1(0, g)
+        copy_w(0, 1, 0)
+        quantize_w(0, 1, 0)
+        gelus(0)
+        for g in (1, 2):
+            copy_w(0, 1, g)
+            quantize_w(0, 1, g)
+        products3_early(0)
+        for b in range(BLOCKS):
+            products3(0, b)
+        copy_w(1, 0, 0)
+        quantize_w(1, 0, 0)
+        multiply(0, 0)
+        multiply(0, 1)
+        products1(1, 0)
+        copy_w(1, 0, 1)
+        quantize_w(1, 0, 1)
+        multiply(0, 2)
+        multiply(0, 3)
+        products1(1, 1)
+        copy_w(1, 0, 2)
+        quantize_h(0, 0, S)
+        quantize_w(1, 0, 2)
+        products1(1, 2)
+        keep_warm(4)
+        copy_w(1, 1, 0)
+        quantize_w(1, 1, 0)
+        gelus(1)
+        keep_warm(4)
+        copy_w(1, 1, 1)
+        quantize_w(1, 1, 1)
+        products3_early(1)
+        keep_warm(4)
+        copy_w(1, 1, 2)
+        quantize_w(1, 1, 2)
+        w2g = keep.tile([P, HALVES * N, PACK], BF16, name="w2g", align_bytes=64)
+        w2q = (
+            keep.tile([P, HALVES * N], U32, name="w2c", align_bytes=64),
+            keep.tile([P, HALVES * N], U8, name="w2s", align_bytes=64),
+        )
+        for q in range(HALVES):
+            interleave(nc, True, w2g[:, q * N : (q + 1) * N, :], w2r[:, q])
+        for b in range(BLOCKS):
+            products3(1, b)
+            multiply(1, b)
+            if b == 1:
+                quantize(nc, w2q[0][:], w2q[1][:], w2g[:])
+            if b >= 1:
+                quantize_h(1, (b - 1) * BLOCK, b * BLOCK)
+        quantize_h(1, (BLOCKS - 1) * BLOCK, S)
+
+        for a in range(2):
+            n0 = a * 256
+            y = psum.tile([P, 256], F32, name="bank")
+            for h in range(HALVES):
+                mm(nc, y[:], w2q, h * N, hq[h], n0, 256, h == 0, h == HALVES - 1)
+            res = keep.tile([P, 256], F32, name=f"res{a}")
+            copy_on(nc, a == 0, res[:], y[:])
+            (nc.sync if a == 0 else nc.scalar).dma_start(out=out[:, n0 : n0 + 256], in_=res[:])

@@ -23,8 +23,20 @@ HALVES = H // HALF
 BLOCK = 128
 BLOCKS = S // BLOCK
 
-X_SCALAR = [(256, 128), (448, 384), (448, 256)]
-W_SCALAR = [96, 96, 32, 16, 16, 48, 48, 64, 96, 32, 0]
+X_SCALAR = [(320, 384), (128, 256), (320, 192)]
+W_SCALAR = {
+    (0, 0, 0): 64,
+    (1, 0, 0): 80,
+    (0, 0, 1): 64,
+    (1, 0, 1): 56,
+    (0, 0, 2): 48,
+    (1, 0, 2): 72,
+    (0, 1, 0): 0,
+    (0, 1, 1): 8,
+    (0, 1, 2): 24,
+    (1, 1, 0): 48,
+    (1, 1, 1): 88,
+}
 
 
 def copy_on(nc, on_scalar, dst, src):
@@ -84,23 +96,30 @@ def tile_picked_pick_glu_gelu_srt_e_kernel(tc, xT, w1, w3, w2, offs, out):
 
         xr = []
         for g in range(PASSES):
-            r = raws.tile([P, PACK, T], F32, name="rawx", bufs=3)
-            nc.sync.dma_start(out=r[:, :, 0:512], in_=x_view[g][:, :, 0:512])
-            nc.sync.dma_start(out=r[:, :, 512:1024], in_=x_view[g][:, :, 512:1024])
+            r = raws.tile([P, PACK, T], F32, name="raw16", bufs=4)
             if g == 0:
+                nc.sync.dma_start(out=r[:, :, 0:512], in_=x_view[g][:, :, 0:512])
+                nc.sync.dma_start(out=r[:, :, 512:1024], in_=x_view[g][:, :, 512:1024])
                 nc.sync.dma_start(out=offsets[:], in_=offs)
-            xr.append(r)
-        chunks = [(h, k, g) for h in range(HALVES) for k in range(2) for g in range(PASSES)]
-        wr = {}
-        for h, k, g in chunks:
-            r = raws.tile([P, PACK, HALF], F32, name="raww", bufs=8)
-            c0 = h * HALF
-            if (h, k, g) == chunks[-1]:
-                nc.sync.dma_start(out=r[:, :, 0:256], in_=w_views[k][g][:, :, c0 : c0 + 256])
-                nc.sync.dma_start(out=r[:, :, 256:512], in_=w_views[k][g][:, :, c0 + 256 : c0 + 512])
             else:
-                nc.sync.dma_start(out=r[:], in_=w_views[k][g][:, :, c0 : c0 + HALF])
-            wr[h, k, g] = r
+                nc.sync.dma_start(out=r[:], in_=x_view[g])
+            xr.append(r)
+        wr = {}
+        for g in range(PASSES):
+            r = raws.tile([P, PACK, H], F32, name="raw16", bufs=4)
+            nc.sync.dma_start(out=r[:], in_=w_views[0][g])
+            for h in range(HALVES):
+                wr[h, 0, g] = r[:, :, h * HALF : (h + 1) * HALF]
+        for h in range(HALVES):
+            for g in range(PASSES):
+                r = raws.tile([P, PACK, HALF], F32, name="raw8", bufs=5)
+                c0 = h * HALF
+                if (h, g) == (HALVES - 1, PASSES - 1):
+                    nc.sync.dma_start(out=r[:, :, 0:256], in_=w_views[1][g][:, :, c0 : c0 + 256])
+                    nc.sync.dma_start(out=r[:, :, 256:512], in_=w_views[1][g][:, :, c0 + 256 : c0 + 512])
+                else:
+                    nc.sync.dma_start(out=r[:], in_=w_views[1][g][:, :, c0 : c0 + HALF])
+                wr[h, 1, g] = r[:]
         w2r = keep.tile([P, HALVES, PACK, N], F32, name="w2r")
         nc.sync.dma_start(out=w2r[:], in_=w2_view)
 
@@ -134,13 +153,13 @@ def tile_picked_pick_glu_gelu_srt_e_kernel(tc, xT, w1, w3, w2, offs, out):
 
         def copy_w(h, k, g):
             grouped = stage.tile([P, HALF, PACK], BF16, name="wg", align_bytes=64, bufs=4)
-            if (h, k, g) == chunks[-1]:
-                splits = [(True, 0, 16), (False, 16, 64), (True, 64, 80), (False, 80, 128)]
+            if (h, k, g) == (1, 1, 2):
+                splits = [(True, 0, 40), (False, 40, 64), (True, 64, 104), (False, 104, 128)]
             else:
-                m = W_SCALAR[chunks.index((h, k, g))]
+                m = W_SCALAR[h, k, g]
                 splits = [(on, a, b) for on, a, b in ((True, 0, m), (False, m, P)) if a < b]
             for on_scalar, m0, m1 in splits:
-                interleave_permuted(nc, on_scalar, grouped[:], wr[h, k, g][:], m0, m1)
+                interleave_permuted(nc, on_scalar, grouped[:], wr[h, k, g], m0, m1)
             wg[h, k, g] = grouped
 
         def quantize_w(h, k, g):
@@ -204,41 +223,29 @@ def tile_picked_pick_glu_gelu_srt_e_kernel(tc, xT, w1, w3, w2, offs, out):
             copy_x(g)
             gather_x(g)
         for g in range(PASSES):
-            copy_w(0, 0, g)
-            quantize_w(0, 0, g)
-            products1(0, g)
+            for h in range(HALVES):
+                copy_w(h, 0, g)
+                quantize_w(h, 0, g)
+                products1(h, g)
+        gelus(0)
         copy_w(0, 1, 0)
         quantize_w(0, 1, 0)
-        gelus(0)
+        gelus(1)
         for g in (1, 2):
             copy_w(0, 1, g)
             quantize_w(0, 1, g)
         products3_early(0)
         for b in range(BLOCKS):
             products3(0, b)
-        copy_w(1, 0, 0)
-        quantize_w(1, 0, 0)
-        multiply(0, 0)
-        multiply(0, 1)
-        products1(1, 0)
-        copy_w(1, 0, 1)
-        quantize_w(1, 0, 1)
-        multiply(0, 2)
-        multiply(0, 3)
-        products1(1, 1)
-        copy_w(1, 0, 2)
-        quantize_h(0, 0, S)
-        quantize_w(1, 0, 2)
-        products1(1, 2)
-        keep_warm(4)
         copy_w(1, 1, 0)
         quantize_w(1, 1, 0)
-        gelus(1)
-        keep_warm(4)
+        for b in range(BLOCKS):
+            multiply(0, b)
         copy_w(1, 1, 1)
         quantize_w(1, 1, 1)
+        quantize_h(0, 0, S)
         products3_early(1)
-        keep_warm(4)
+        keep_warm(6)
         copy_w(1, 1, 2)
         quantize_w(1, 1, 2)
         w2g = keep.tile([P, HALVES * N, PACK], BF16, name="w2g", align_bytes=64)

@@ -23,19 +23,19 @@ HALVES = H // HALF
 BLOCK = 128
 BLOCKS = S // BLOCK
 
-X_SCALAR = [(320, 384), (128, 256), (320, 192)]
+X_SCALAR = [(448, 384), (512, 384), (128, 448)]
 W_SCALAR = {
-    (0, 0, 0): 64,
-    (1, 0, 0): 80,
-    (0, 0, 1): 64,
-    (1, 0, 1): 56,
-    (0, 0, 2): 48,
-    (1, 0, 2): 72,
+    (0, 0, 0): 128,
+    (1, 0, 0): 32,
+    (0, 0, 1): 72,
+    (1, 0, 1): 96,
+    (0, 0, 2): 64,
+    (1, 0, 2): 48,
     (0, 1, 0): 0,
-    (0, 1, 1): 8,
-    (0, 1, 2): 24,
-    (1, 1, 0): 48,
-    (1, 1, 1): 88,
+    (0, 1, 1): 0,
+    (0, 1, 2): 64,
+    (1, 1, 0): 56,
+    (1, 1, 1): 64,
 }
 
 
@@ -97,12 +97,9 @@ def tile_picked_pick_glu_gelu_srt_e_kernel(tc, xT, w1, w3, w2, offs, out):
         xr = []
         for g in range(PASSES):
             r = raws.tile([P, PACK, T], F32, name="raw16", bufs=4)
+            nc.sync.dma_start(out=r[:], in_=x_view[g])
             if g == 0:
-                nc.sync.dma_start(out=r[:, :, 0:512], in_=x_view[g][:, :, 0:512])
-                nc.sync.dma_start(out=r[:, :, 512:1024], in_=x_view[g][:, :, 512:1024])
                 nc.sync.dma_start(out=offsets[:], in_=offs)
-            else:
-                nc.sync.dma_start(out=r[:], in_=x_view[g])
             xr.append(r)
         wr = {}
         for g in range(PASSES):
@@ -137,8 +134,10 @@ def tile_picked_pick_glu_gelu_srt_e_kernel(tc, xT, w1, w3, w2, offs, out):
             grouped = stage.tile([P, T, PACK], BF16, name="xg", align_bytes=64, bufs=2)
             for a in range(0, T, 512):
                 b = a + X_SCALAR[g][a // 512]
-                interleave(nc, True, grouped[:, a:b, :], xr[g][:, :, a:b])
-                interleave(nc, False, grouped[:, b : a + 512, :], xr[g][:, :, b : a + 512])
+                for on_scalar, n0, n1 in ((True, a, b), (False, b, a + 512)):
+                    if n0 < n1:
+                        interleave(nc, on_scalar, grouped[:, n0:n1, :], xr[g][:, :, n0:n1])
+            for a in range(0, T, 512):
                 quantize(nc, words[g][:, a : a + 512], bytes8[g][:, a : a + 512], grouped[:, a : a + 512, :])
 
         def gather_x(g):
@@ -154,7 +153,7 @@ def tile_picked_pick_glu_gelu_srt_e_kernel(tc, xT, w1, w3, w2, offs, out):
         def copy_w(h, k, g):
             grouped = stage.tile([P, HALF, PACK], BF16, name="wg", align_bytes=64, bufs=4)
             if (h, k, g) == (1, 1, 2):
-                splits = [(True, 0, 40), (False, 40, 64), (True, 64, 104), (False, 104, 128)]
+                splits = [(True, 0, 56), (False, 56, 64), (True, 64, 112), (False, 112, 128)]
             else:
                 m = W_SCALAR[h, k, g]
                 splits = [(on, a, b) for on, a, b in ((True, 0, m), (False, m, P)) if a < b]
@@ -185,11 +184,11 @@ def tile_picked_pick_glu_gelu_srt_e_kernel(tc, xT, w1, w3, w2, offs, out):
             for t in range(PACK):
                 nc.scalar.activation(gate[h][:, t, :], acc[h, t][:], GELU)
 
-        def products3_early(h):
+        def products3_early(h, g):
             for b in range(BLOCKS):
-                banks[h, b] = psum.tile([P, PACK, BLOCK], F32, name="bank")
-                for g in range(PASSES - 1):
-                    mm(nc, banks[h, b][:, 0, :], wq[h, 1, g], 0, picked[g], b * BLOCK, BLOCK, g == 0, False)
+                if g == 0:
+                    banks[h, b] = psum.tile([P, PACK, BLOCK], F32, name="bank")
+                mm(nc, banks[h, b][:, 0, :], wq[h, 1, g], 0, picked[g], b * BLOCK, BLOCK, g == 0, False)
 
         def products3(h, b):
             for t in range(PACK):
@@ -225,29 +224,36 @@ def tile_picked_pick_glu_gelu_srt_e_kernel(tc, xT, w1, w3, w2, offs, out):
         for g in range(PASSES):
             for h in range(HALVES):
                 copy_w(h, 0, g)
+            for h in range(HALVES):
                 quantize_w(h, 0, g)
                 products1(h, g)
         gelus(0)
         copy_w(0, 1, 0)
         quantize_w(0, 1, 0)
+        products3_early(0, 0)
         gelus(1)
-        for g in (1, 2):
-            copy_w(0, 1, g)
-            quantize_w(0, 1, g)
-        products3_early(0)
+        copy_w(0, 1, 1)
+        quantize_w(0, 1, 1)
+        products3_early(0, 1)
+        copy_w(0, 1, 2)
+        quantize_w(0, 1, 2)
         for b in range(BLOCKS):
             products3(0, b)
         copy_w(1, 1, 0)
         quantize_w(1, 1, 0)
-        for b in range(BLOCKS):
-            multiply(0, b)
+        products3_early(1, 0)
+        keep_warm(2)
+        multiply(0, 0)
+        multiply(0, 1)
         copy_w(1, 1, 1)
         quantize_w(1, 1, 1)
-        quantize_h(0, 0, S)
-        products3_early(1)
-        keep_warm(6)
+        products3_early(1, 1)
+        keep_warm(3)
+        multiply(0, 2)
+        multiply(0, 3)
         copy_w(1, 1, 2)
         quantize_w(1, 1, 2)
+        quantize_h(0, 0, S)
         w2g = keep.tile([P, HALVES * N, PACK], BF16, name="w2g", align_bytes=64)
         w2q = (
             keep.tile([P, HALVES * N], U32, name="w2c", align_bytes=64),
@@ -255,20 +261,18 @@ def tile_picked_pick_glu_gelu_srt_e_kernel(tc, xT, w1, w3, w2, offs, out):
         )
         for q in range(HALVES):
             interleave(nc, True, w2g[:, q * N : (q + 1) * N, :], w2r[:, q])
+        quantize(nc, w2q[0][:], w2q[1][:], w2g[:])
         for b in range(BLOCKS):
             products3(1, b)
             multiply(1, b)
-            if b == 1:
-                quantize(nc, w2q[0][:], w2q[1][:], w2g[:])
             if b >= 1:
                 quantize_h(1, (b - 1) * BLOCK, b * BLOCK)
         quantize_h(1, (BLOCKS - 1) * BLOCK, S)
 
-        for a in range(2):
-            n0 = a * 256
+        for a, (n0, n) in enumerate(((0, 256), (256, 128), (384, 128))):
             y = psum.tile([P, 256], F32, name="bank")
             for h in range(HALVES):
-                mm(nc, y[:], w2q, h * N, hq[h], n0, 256, h == 0, h == HALVES - 1)
-            res = keep.tile([P, 256], F32, name=f"res{a}")
-            copy_on(nc, a == 0, res[:], y[:])
-            (nc.sync if a == 0 else nc.scalar).dma_start(out=out[:, n0 : n0 + 256], in_=res[:])
+                mm(nc, y[:, 0:n], w2q, h * N, hq[h], n0, n, h == 0, h == HALVES - 1)
+            res = keep.tile([P, n], F32, name=f"res{a}")
+            copy_on(nc, a < 2, res[:], y[:, 0:n])
+            nc.sync.dma_start(out=out[:, n0 : n0 + n], in_=res[:])

@@ -23,19 +23,19 @@ HALVES = H // HALF
 BLOCK = 128
 BLOCKS = S // BLOCK
 
-X_SCALAR = [(448, 384), (512, 384), (128, 448)]
+X_SCALAR = [(384, 512), (256, 448), (128, 320)]
 W_SCALAR = {
-    (0, 0, 0): 128,
-    (1, 0, 0): 32,
-    (0, 0, 1): 72,
-    (1, 0, 1): 96,
+    (0, 0, 0): 24,
+    (1, 0, 0): 120,
+    (0, 0, 1): 32,
+    (1, 0, 1): 88,
     (0, 0, 2): 64,
     (1, 0, 2): 48,
-    (0, 1, 0): 0,
-    (0, 1, 1): 0,
-    (0, 1, 2): 64,
-    (1, 1, 0): 56,
-    (1, 1, 1): 64,
+    (1, 1, 0): 8,
+    (0, 1, 0): 64,
+    (0, 1, 1): 8,
+    (0, 1, 2): 72,
+    (1, 1, 1): 48,
 }
 
 
@@ -107,9 +107,13 @@ def tile_picked_pick_glu_gelu_srt_e_kernel(tc, xT, w1, w3, w2, offs, out):
             nc.sync.dma_start(out=r[:], in_=w_views[0][g])
             for h in range(HALVES):
                 wr[h, 0, g] = r[:, :, h * HALF : (h + 1) * HALF]
+        r = raws.tile([P, PACK, H], F32, name="raw16", bufs=4)
+        nc.sync.dma_start(out=r[:], in_=w_views[1][0])
         for h in range(HALVES):
-            for g in range(PASSES):
-                r = raws.tile([P, PACK, HALF], F32, name="raw8", bufs=5)
+            wr[h, 1, 0] = r[:, :, h * HALF : (h + 1) * HALF]
+        for h in range(HALVES):
+            for g in range(1, PASSES):
+                r = raws.tile([P, PACK, HALF], F32, name="raw8", bufs=4)
                 c0 = h * HALF
                 if (h, g) == (HALVES - 1, PASSES - 1):
                     nc.sync.dma_start(out=r[:, :, 0:256], in_=w_views[1][g][:, :, c0 : c0 + 256])
@@ -153,7 +157,7 @@ def tile_picked_pick_glu_gelu_srt_e_kernel(tc, xT, w1, w3, w2, offs, out):
         def copy_w(h, k, g):
             grouped = stage.tile([P, HALF, PACK], BF16, name="wg", align_bytes=64, bufs=4)
             if (h, k, g) == (1, 1, 2):
-                splits = [(True, 0, 56), (False, 56, 64), (True, 64, 112), (False, 112, 128)]
+                splits = [(True, 0, 64), (True, 64, 120), (False, 120, 128)]
             else:
                 m = W_SCALAR[h, k, g]
                 splits = [(on, a, b) for on, a, b in ((True, 0, m), (False, m, P)) if a < b]
@@ -228,32 +232,31 @@ def tile_picked_pick_glu_gelu_srt_e_kernel(tc, xT, w1, w3, w2, offs, out):
                 quantize_w(h, 0, g)
                 products1(h, g)
         gelus(0)
+        copy_w(1, 1, 0)
         copy_w(0, 1, 0)
+        quantize_w(1, 1, 0)
         quantize_w(0, 1, 0)
         products3_early(0, 0)
         gelus(1)
         copy_w(0, 1, 1)
         quantize_w(0, 1, 1)
         products3_early(0, 1)
+        products3_early(1, 0)
         copy_w(0, 1, 2)
         quantize_w(0, 1, 2)
-        for b in range(BLOCKS):
-            products3(0, b)
-        copy_w(1, 1, 0)
-        quantize_w(1, 1, 0)
-        products3_early(1, 0)
-        keep_warm(2)
-        multiply(0, 0)
-        multiply(0, 1)
+        products3(0, 0)
+        products3(0, 1)
         copy_w(1, 1, 1)
+        products3(0, 2)
+        multiply(0, 0)
         quantize_w(1, 1, 1)
         products3_early(1, 1)
-        keep_warm(3)
+        multiply(0, 1)
+        products3(0, 3)
+        keep_warm(2)
+        copy_w(1, 1, 2)
         multiply(0, 2)
         multiply(0, 3)
-        copy_w(1, 1, 2)
-        quantize_w(1, 1, 2)
-        quantize_h(0, 0, S)
         w2g = keep.tile([P, HALVES * N, PACK], BF16, name="w2g", align_bytes=64)
         w2q = (
             keep.tile([P, HALVES * N], U32, name="w2c", align_bytes=64),
@@ -261,6 +264,8 @@ def tile_picked_pick_glu_gelu_srt_e_kernel(tc, xT, w1, w3, w2, offs, out):
         )
         for q in range(HALVES):
             interleave(nc, True, w2g[:, q * N : (q + 1) * N, :], w2r[:, q])
+        quantize_w(1, 1, 2)
+        quantize_h(0, 0, S)
         quantize(nc, w2q[0][:], w2q[1][:], w2g[:])
         for b in range(BLOCKS):
             products3(1, b)

from contextlib import ExitStack

import concourse.mybir as mybir

K, T, S, H, N = 1536, 1024, 512, 1024, 128
FLOPS = 2 * K * H * S * 2 + 2 * H * N * S

F32 = mybir.dt.float32
BF16 = mybir.dt.bfloat16
U32 = mybir.dt.uint32
U16 = mybir.dt.uint16
U8 = mybir.dt.uint8
FP8X4 = mybir.dt.float8_e4m3fn_x4
MULT = mybir.AluOpType.mult
GELU = mybir.ActivationFunctionType.Gelu_apprx_tanh

P = 128
PACK = 4
K_PASS = P * PACK
PASSES = K // K_PASS
HALF = 512
HALVES = H // HALF
BLOCK = 128
BLOCKS = S // BLOCK

X_SCALAR = [(384, 512), (256, 448), (128, 320)]
W_SCALAR = {
    (0, 0, 0): 24,
    (1, 0, 0): 120,
    (0, 0, 1): 32,
    (1, 0, 1): 88,
    (0, 0, 2): 64,
    (1, 0, 2): 48,
    (1, 1, 0): 8,
    (0, 1, 0): 64,
    (0, 1, 1): 8,
    (0, 1, 2): 72,
    (1, 1, 1): 48,
}


def copy_on(nc, on_scalar, dst, src):
    if on_scalar:
        nc.scalar.copy(out=dst, in_=src)
    else:
        nc.vector.tensor_copy(out=dst, in_=src)


def interleave(nc, on_scalar, dst, src):
    copy_on(
        nc,
        on_scalar,
        dst.rearrange("p (c i) j -> p c j i", i=4),
        src.rearrange("p j (c i) -> p c j i", i=4),
    )


def interleave_permuted(nc, on_scalar, dst, src, m0, m1):
    copy_on(
        nc,
        on_scalar,
        dst.rearrange("p (t m) j -> p m j t", t=4)[:, m0:m1],
        src.rearrange("p j (m t) -> p m j t", t=4)[:, m0:m1],
    )


def quantize(nc, codes, scales, grouped):
    nc.vector.quantize_mx(out=codes.bitcast(FP8X4), scales=scales, in_=grouped.rearrange("p w j -> p (w j)"))


def mm(nc, out, w, col, x, n0, n, start, stop):
    nc.tensor.matmul_mx(
        out=out,
        lhsT=w[0][:, col : col + P].bitcast(FP8X4),
        lhsT_scale=w[1][:, col : col + P],
        rhs=x[0][:, n0 : n0 + n].bitcast(FP8X4),
        rhs_scale=x[1][:, n0 : n0 + n],
        start=start,
        stop=stop,
    )


def tile_picked_pick_glu_gelu_srt_e_kernel(tc, xT, w1, w3, w2, offs, out):
    nc = tc.nc
    with ExitStack() as ctx:
        keep = ctx.enter_context(tc.tile_pool(name="keep", bufs=1))
        raws = ctx.enter_context(tc.tile_pool(name="raws", bufs=1))
        stage = ctx.enter_context(tc.tile_pool(name="stage", bufs=3))
        psum = ctx.enter_context(tc.psum_pool(name="psum", bufs=8))

        offsets = keep.tile([P, S // 16], U16, name="offsets")

        x_view = xT.rearrange("(g p j) c -> g p j c", g=PASSES, j=PACK)
        w_views = [w.rearrange("(g p j) c -> g p j c", g=PASSES, j=PACK) for w in (w1, w3)]
        w2_view = w2.rearrange("(g p j) c -> p g j c", g=HALVES, j=PACK)

        xr = []
        for g in range(PASSES):
            r = raws.tile([P, PACK, T], F32, name="raw16", bufs=4)
            nc.sync.dma_start(out=r[:], in_=x_view[g])
            if g == 0:
                nc.sync.dma_start(out=offsets[:], in_=offs)
            xr.append(r)
        wr = {}
        for g in range(PASSES):
            r = raws.tile([P, PACK, H], F32, name="raw16", bufs=4)
            nc.sync.dma_start(out=r[:], in_=w_views[0][g])
            for h in range(HALVES):
                wr[h, 0, g] = r[:, :, h * HALF : (h + 1) * HALF]
        r = raws.tile([P, PACK, H], F32, name="raw16", bufs=4)
        nc.sync.dma_start(out=r[:], in_=w_views[1][0])
        for h in range(HALVES):
            wr[h, 1, 0] = r[:, :, h * HALF : (h + 1) * HALF]
        for h in range(HALVES):
            for g in range(1, PASSES):
                r = raws.tile([P, PACK, HALF], F32, name="raw8", bufs=4)
                c0 = h * HALF
                if (h, g) == (HALVES - 1, PASSES - 1):
                    nc.sync.dma_start(out=r[:, :, 0:256], in_=w_views[1][g][:, :, c0 : c0 + 256])
                    nc.sync.dma_start(out=r[:, :, 256:512], in_=w_views[1][g][:, :, c0 + 256 : c0 + 512])
                else:
                    nc.sync.dma_start(out=r[:], in_=w_views[1][g][:, :, c0 : c0 + HALF])
                wr[h, 1, g] = r[:]
        w2r = keep.tile([P, HALVES, PACK, N], F32, name="w2r")
        nc.sync.dma_start(out=w2r[:], in_=w2_view)

        warm = keep.tile([P, 1], F32, name="warm")
        nc.vector.memset(warm[:], 0.0)
        nc.scalar.activation(warm[:], warm[:], GELU)

        words, bytes8, picked = [], [], []
        for g in range(PASSES):
            words.append(keep.tile([P, T], U32, name=f"words{g}", align_bytes=64))
            bytes8.append(keep.tile([P, T], U8, name=f"bytes{g}", align_bytes=64))
            nc.gpsimd.memset(bytes8[g][:], 0)

        def copy_x(g):
            grouped = stage.tile([P, T, PACK], BF16, name="xg", align_bytes=64, bufs=2)
            for a in range(0, T, 512):
                b = a + X_SCALAR[g][a // 512]
                for on_scalar, n0, n1 in ((True, a, b), (False, b, a + 512)):
                    if n0 < n1:
                        interleave(nc, on_scalar, grouped[:, n0:n1, :], xr[g][:, :, n0:n1])
            for a in range(0, T, 512):
                quantize(nc, words[g][:, a : a + 512], bytes8[g][:, a : a + 512], grouped[:, a : a + 512, :])

        def gather_x(g):
            gw = keep.tile([P, S], U32, name=f"pw{g}", align_bytes=64)
            gs = keep.tile([P, S], U8, name=f"ps{g}", align_bytes=64)
            nc.vector.tensor_copy(gw[:], words[g][:].indirect(offsets[:]))
            nc.vector.tensor_copy(gs[:], bytes8[g][:].indirect(offsets[:]))
            picked.append((gw, gs))

        wg = {}
        wq = {}

        def copy_w(h, k, g):
            grouped = stage.tile([P, HALF, PACK], BF16, name="wg", align_bytes=64, bufs=4)
            if (h, k, g) == (1, 1, 2):
                splits = [(True, 0, 64), (True, 64, 120), (False, 120, 128)]
            else:
                m = W_SCALAR[h, k, g]
                splits = [(on, a, b) for on, a, b in ((True, 0, m), (False, m, P)) if a < b]
            for on_scalar, m0, m1 in splits:
                interleave_permuted(nc, on_scalar, grouped[:], wr[h, k, g], m0, m1)
            wg[h, k, g] = grouped

        def quantize_w(h, k, g):
            codes = keep.tile([P, HALF], U32, name=f"wc{h}{k}{g}", align_bytes=64)
            scales = keep.tile([P, HALF], U8, name=f"ws{h}{k}{g}", align_bytes=64)
            quantize(nc, codes[:], scales[:], wg[h, k, g][:])
            wq[h, k, g] = (codes, scales)

        acc = {}
        gate = {}
        banks = {}
        hg = {}
        hq = {}

        def products1(h, g):
            for t in range(PACK):
                if g == 0:
                    acc[h, t] = psum.tile([P, S], F32, name="bank")
                mm(nc, acc[h, t][:], wq[h, 0, g], t * P, picked[g], 0, S, g == 0, g == PASSES - 1)

        def gelus(h):
            gate[h] = keep.tile([P, PACK, S], F32, name=f"gate{h}")
            for t in range(PACK):
                nc.scalar.activation(gate[h][:, t, :], acc[h, t][:], GELU)

        def products3_early(h, g):
            for b in range(BLOCKS):
                if g == 0:
                    banks[h, b] = psum.tile([P, PACK, BLOCK], F32, name="bank")
                mm(nc, banks[h, b][:, 0, :], wq[h, 1, g], 0, picked[g], b * BLOCK, BLOCK, g == 0, False)

        def products3(h, b):
            for t in range(PACK):
                for g in range(PASSES - 1 if t == 0 else 0, PASSES):
                    mm(nc, banks[h, b][:, t, :], wq[h, 1, g], t * P, picked[g], b * BLOCK, BLOCK, g == 0, g == PASSES - 1)

        def multiply(h, b):
            n = slice(b * BLOCK, (b + 1) * BLOCK)
            if b == 0:
                hg[h] = keep.tile([P, S, PACK], BF16, name=f"hg{h}", align_bytes=64)
                hq[h] = (
                    keep.tile([P, S], U32, name=f"hc{h}", align_bytes=64),
                    keep.tile([P, S], U8, name=f"hs{h}", align_bytes=64),
                )
            nc.vector.tensor_tensor(
                hg[h][:, n, :],
                banks[h, b][:].rearrange("p t n -> p n t"),
                gate[h][:, :, n].rearrange("p t n -> p n t"),
                MULT,
            )

        def quantize_h(h, n0, n1):
            quantize(nc, hq[h][0][:, n0:n1], hq[h][1][:, n0:n1], hg[h][:, n0:n1, :])

        def keep_warm(n):
            bank = psum.tile([P, S], F32, name="bank")
            for _ in range(n):
                mm(nc, bank[:], wq[1, 0, 0], 0, picked[0], 0, S, True, True)

        for g in range(PASSES):
            copy_x(g)
            gather_x(g)
        for g in range(PASSES):
            for h in range(HALVES):
                copy_w(h, 0, g)
            for h in range(HALVES):
                quantize_w(h, 0, g)
                products1(h, g)
        gelus(0)
        copy_w(1, 1, 0)
        copy_w(0, 1, 0)
        quantize_w(1, 1, 0)
        quantize_w(0, 1, 0)
        products3_early(0, 0)
        gelus(1)
        copy_w(0, 1, 1)
        quantize_w(0, 1, 1)
        products3_early(0, 1)
        products3_early(1, 0)
        copy_w(0, 1, 2)
        quantize_w(0, 1, 2)
        products3(0, 0)
        products3(0, 1)
        copy_w(1, 1, 1)
        products3(0, 2)
        multiply(0, 0)
        quantize_w(1, 1, 1)
        products3_early(1, 1)
        multiply(0, 1)
        products3(0, 3)
        keep_warm(2)
        copy_w(1, 1, 2)
        multiply(0, 2)
        multiply(0, 3)
        w2g = keep.tile([P, HALVES * N, PACK], BF16, name="w2g", align_bytes=64)
        w2q = (
            keep.tile([P, HALVES * N], U32, name="w2c", align_bytes=64),
            keep.tile([P, HALVES * N], U8, name="w2s", align_bytes=64),
        )
        for q in range(HALVES):
            interleave(nc, True, w2g[:, q * N : (q + 1) * N, :], w2r[:, q])
        quantize_w(1, 1, 2)
        quantize_h(0, 0, S)
        quantize(nc, w2q[0][:], w2q[1][:], w2g[:])
        for b in range(BLOCKS):
            products3(1, b)
            multiply(1, b)
            if b >= 1:
                quantize_h(1, (b - 1) * BLOCK, b * BLOCK)
        quantize_h(1, (BLOCKS - 1) * BLOCK, S)

        for a, (n0, n) in enumerate(((0, 256), (256, 128), (384, 128))):
            y = psum.tile([P, 256], F32, name="bank")
            for h in range(HALVES):
                mm(nc, y[:, 0:n], w2q, h * N, hq[h], n0, n, h == 0, h == HALVES - 1)
            res = keep.tile([P, n], F32, name=f"res{a}")
            copy_on(nc, a < 2, res[:], y[:, 0:n])
            nc.sync.dma_start(out=out[:, n0 : n0 + n], in_=res[:])
